import numpy as np
import ml_dtypes


def mxq(x, axis, fmt="e4m3"):
    dtype, down = {"e4m3": (ml_dtypes.float8_e4m3fn, 7), "e5m2": (ml_dtypes.float8_e5m2, 14)}[fmt]
    v = np.moveaxis(np.asarray(x, np.float32).astype(ml_dtypes.bfloat16).astype(np.float64), axis, -1)
    blocks = v.reshape(v.shape[:-1] + (-1, 32))
    amax = np.abs(blocks).max(-1, keepdims=True)
    byte = np.maximum(np.where(amax > 0, np.frexp(amax)[1] - 1 + 127, 0) - down, 1)
    scale = np.exp2(byte - 127.0)
    codes = (blocks / scale).astype(np.float32).astype(dtype).astype(np.float64)
    return np.moveaxis((codes * scale).reshape(v.shape), -1, axis)


WIDE = False


def mx_kscale(k):
    if not WIDE:
        return np.ones(k)
    levels = np.array([10, -10, 5, -5, 0])
    if k % 512:
        return np.exp2(np.random.permutation(np.resize(levels, k // 32))).repeat(32)
    a = np.empty((k // 512, 16))
    for p in range(k // 512):
        a[p, :8] = np.random.permutation(np.resize(levels, 8))
        for g in range(8):
            far = levels[np.abs(levels - a[p, g]) >= 10]
            a[p, g + 8] = far[np.random.randint(len(far))]
    return np.exp2(a.ravel()).repeat(32)


BF16 = ml_dtypes.bfloat16


def bf(x):
    return np.asarray(x, np.float32).astype(BF16)


def f64(x):
    return np.asarray(x).astype(np.float64)


E2M1 = np.array([0.0, 0.5, 1.0, 1.5, 2.0, 3.0, 4.0, 6.0, -0.0, -0.5, -1.0, -1.5, -2.0, -3.0, -4.0, -6.0])


def pack_weight(w, fmt):
    k, n = w.shape
    w = f64(bf(w)).reshape(k // 32, 32, n)
    amax = np.abs(w).max(1)
    if fmt == "e4m3":
        byte = np.frexp(amax)[1] - 1 + 127 - 7
    else:
        mant, ex = np.frexp(amax / 6.0)
        byte = np.where(mant > 0.5, ex, ex - 1) + 127
    byte = np.clip(np.where(amax > 0, byte, 1), 1, 254)
    scaled = (w * np.exp2(127.0 - byte)[:, None, :]).reshape(k, n).astype(np.float32)
    by_word = np.ascontiguousarray(scaled.reshape(k // 512, 128, 4, n).transpose(0, 1, 3, 2))
    if fmt == "e4m3":
        words = by_word.astype(ml_dtypes.float8_e4m3fn).view(np.uint8)
    else:
        c = by_word.astype(ml_dtypes.float4_e2m1fn).view(np.uint8) & 0xF
        words = c[..., 0::2] | (c[..., 1::2] << 4)
    return np.ascontiguousarray(words), np.ascontiguousarray(byte.astype(np.uint8).reshape(k // 512, 16, n))


def unpack_weight(words, scales, fmt):
    g, p, n, _ = words.shape
    if fmt == "e4m3":
        vals = np.ascontiguousarray(words).view(ml_dtypes.float8_e4m3fn).astype(np.float64)
    else:
        nib = np.empty((g, p, n, 4), np.uint8)
        nib[..., 0::2] = words & 0xF
        nib[..., 1::2] = words >> 4
        vals = E2M1[nib]
    vals = vals * np.repeat(np.exp2(scales.astype(np.float64) - 127.0), 8, axis=1)[..., None]
    return vals.transpose(0, 1, 3, 2).reshape(g * 512, n)
def pack4(w):
    words, scales = pack_weight(w, "e2m1")
    return words.reshape(words.shape[0], 128, -1), scales


def unpack4(words, scales):
    return unpack_weight(words.reshape(words.shape[0], 128, -1, 2), scales, "e2m1")


M, K, N = 512, 2048, 1024


def setup_inputs():
    s = mx_kscale(K)
    z = np.random.standard_t(5, (M, K)) * s ** 2
    a = np.random.standard_t(5, (K, N)) / np.sqrt(K) / s[:, None]
    b = np.random.standard_t(5, (K, N)) / np.sqrt(K) / s[:, None]
    x = np.random.standard_t(5, (N, K)) / np.sqrt(K) / s
    a_words, a_scales = pack4(a)
    b_words, b_scales = pack_weight(b, "e4m3")
    return {"z": bf(z),
            "a_words": a_words, "a_scales": a_scales,
            "b_words": b_words, "b_scales": b_scales,
            "x": bf(x)}


def reference(z, a_words, a_scales, b_words, b_scales, x):
    z = f64(z)
    y = np.sign(z) * np.sqrt(np.abs(z))
    yq = mxq(y, 1, "e4m3")
    ca = yq @ unpack4(a_words, a_scales)
    cb = yq @ unpack_weight(b_words, b_scales, "e4m3")
    cx = yq @ mxq(f64(x), 1, "e4m3").T
    return ca * cb + cx

@@ -1,0 +1,320 @@
+from contextlib import ExitStack
+
+import concourse.mybir as mybir
+from concourse.masks import make_identity
+
+M, K, N = 512, 2048, 1024
+FLOPS = 3 * 2 * M * K * N
+
+F32 = mybir.dt.float32
+BF16 = mybir.dt.bfloat16
+I32 = mybir.dt.int32
+U32 = mybir.dt.uint32
+U8 = mybir.dt.uint8
+FP8X4 = mybir.dt.float8_e4m3fn_x4
+FP4X4 = mybir.dt.float4_e2m1fn_x4
+ALU = mybir.AluOpType
+ACT = mybir.ActivationFunctionType
+
+P = 128
+PASSES = K // 512
+HALF = 512
+M_TILES = M // P
+X_TILES = N // P
+TURN_BANKS = 4
+SUM_BANKS = 4
+FINITE = 2.0 ** 100
+
+
+def tile_fractional_covariance_product_s10_kernel(tc, z, a_words, a_scales, b_words, b_scales, x, out):
+    nc = tc.nc
+    with ExitStack() as ctx:
+        keep = ctx.enter_context(tc.tile_pool(name="keep", bufs=1))
+        stage = ctx.enter_context(tc.tile_pool(name="stage", bufs=4))
+        psum = ctx.enter_context(tc.psum_pool(name="psum", bufs=1))
+        ctx.enter_context(tc.manual_schedule())
+
+        ident = keep.tile([P, P], F32, name="ident")
+        make_identity(nc, ident[:])
+
+        a_plane = []
+        for c in range(2):
+            plane = keep.tile([P, 2, N], U8, name="a_plane%d" % c, align_bytes=64)
+            a_plane.append(plane)
+        b_plane = keep.tile([P, N], U8, name="b_plane", align_bytes=64)
+        one = keep.tile([P, 8], F32, name="one")
+        nc.vector.memset(one[:], 1.0)
+        nc.vector.memset(a_plane[0][:].rearrange("p g n -> p (g n)").bitcast(I32), 0)
+        nc.vector.memset(a_plane[1][:].rearrange("p g n -> p (g n)").bitcast(I32), 0)
+        nc.vector.memset(b_plane[:].bitcast(I32), 0)
+        warm = keep.tile([P, 8], F32, name="warm")
+        nc.scalar.activation(out=warm[:], in_=one[:], func=ACT.Abs_reciprocal_sqrt)
+
+        z_raw, x_raw, a_codes, b_codes = {}, {}, {}, {}
+
+        def load_z(i, g0, ng):
+            raw = keep.tile([P, ng * 512], BF16, name="z%d_%d" % (i, g0), align_bytes=64)
+            nc.sync.dma_start(out=raw[:], in_=z[i * P:(i + 1) * P, g0 * 512:(g0 + ng) * 512])
+            for g in range(ng):
+                z_raw[i, g0 + g] = (raw, g)
+
+        def load_x(j):
+            raw = keep.tile([P, K], BF16, name="x%d" % j, align_bytes=64)
+            nc.sync.dma_start(out=raw[:], in_=x[j * P:(j + 1) * P, :])
+            x_raw[j] = raw
+
+        def load_a_scales(c):
+            rows = a_scales.rearrange("g (q r) n -> r q g n", r=4)
+            for r in range(4):
+                nc.sync.dma_start(out=a_plane[c][r:P:32, :, :].bitcast(I32),
+                                  in_=rows[r][:, 2 * c:2 * c + 2, :].bitcast(I32))
+
+        def load_a(g):
+            codes = keep.tile([P, 2 * N], U8, name="a_codes%d" % g, align_bytes=64)
+            nc.sync.dma_start(out=codes[:].bitcast(I32), in_=a_words[g].bitcast(I32))
+            a_codes[g] = codes
+
+        def load_b_scales():
+            for q in range(4):
+                nc.sync.dma_start(out=b_plane[32 * q:32 * q + 16, :].bitcast(I32),
+                                  in_=b_scales[:, 4 * q:4 * q + 4, :].bitcast(I32))
+
+        def load_b(h):
+            words = b_words.rearrange("g p n t -> p g (n t)")
+            for c in range(2):
+                codes = keep.tile([P, 2, HALF], U32, name="b_codes%d_%d" % (h, c), align_bytes=64)
+                nc.sync.dma_start(out=codes[:].bitcast(I32),
+                                  in_=words[:, 2 * c:2 * c + 2, 4 * h * HALF:4 * (h + 1) * HALF].bitcast(I32))
+                b_codes[h, c] = codes
+
+        load_z(0, 0, 1)
+        load_z(0, 1, 1)
+        load_z(0, 2, 2)
+        load_a_scales(0)
+        load_a(0)
+        load_a(1)
+        load_z(1, 0, 2)
+        load_a_scales(1)
+        load_a(2)
+        load_z(1, 2, 2)
+        load_a(3)
+        load_z(2, 0, 4)
+        load_b_scales()
+        load_b(0)
+        load_b(1)
+        load_z(3, 0, 4)
+        for j in range(X_TILES):
+            load_x(j)
+
+        y_codes, y_plane = [], []
+        for i in range(M_TILES):
+            codes = keep.tile([P, PASSES * P], U32, name="y_codes%d" % i, align_bytes=64)
+            plane = keep.tile([P, PASSES * P], U8, name="y_plane%d" % i, align_bytes=64)
+            y_codes.append(codes)
+            y_plane.append(plane)
+        x_codes, x_plane = {}, {}
+        for h in range(2):
+            for g in range(PASSES):
+                codes = keep.tile([P, HALF], U32, name="x_codes%d_%d" % (h, g), align_bytes=64)
+                plane = keep.tile([P, HALF], U8, name="x_plane%d_%d" % (h, g), align_bytes=64)
+                x_codes[h, g] = codes
+                x_plane[h, g] = plane
+
+        turn_count, sum_count = [], []
+        roots, y_sorted, x_sorted, turned, grouped, sums, partial = {}, {}, {}, {}, {}, {}, {}
+
+        def turn_bank(index):
+            return psum.tile([P, 2, 2, P], F32, name="bank%d" % index)
+
+        def z_view(i, g0, ng):
+            raw, first = z_raw[i, g0]
+            return raw[:, first * 512:(first + ng) * 512].rearrange("p (q u e) -> p u q e", u=2, e=2)
+
+        def root(i, g0, ng):
+            r = stage.tile([P, 2, ng * P, 2], F32, name="root", align_bytes=64)
+            nc.scalar.activation(out=r[:], in_=z_view(i, g0, ng), func=ACT.Abs_reciprocal_sqrt)
+            roots[i, g0] = r
+
+        def power(i, g0, ng):
+            y = stage.tile([P, 2, ng * P, 2], BF16, name="y_sorted", align_bytes=64)
+            for u in range(2):
+                nc.vector.scalar_tensor_tensor(out=y[:, u], in0=roots[i, g0][:, u], scalar=FINITE,
+                                               in1=z_view(i, g0, ng)[:, u], op0=ALU.min, op1=ALU.mult)
+            y_sorted[i, g0] = y
+
+        def turn_y(i, g0, ng):
+            bank = turn_bank(len(turn_count) % 3)
+            turn_count.append(bank)
+            words = y_sorted[i, g0][:].rearrange("p u q e -> p u (q e)").bitcast(F32)
+            for g in range(ng):
+                for u in range(2):
+                    nc.tensor.transpose(bank[:, g, u, :], words[:, u, g * P:(g + 1) * P], ident[:])
+            turned["y", i, g0] = (bank, ng)
+
+        def copy_out(key):
+            bank, count = turned[key]
+            tile = stage.tile([P, count, P, 2], F32, name="grouped", bufs=6, align_bytes=64)
+            nc.scalar.copy(out=tile[:], in_=bank[:, 0:count].rearrange("p a u r -> p a r u"))
+            grouped[key] = tile
+
+        def quantize(key, codes, plane):
+            nc.vector.quantize_mx(out=codes.bitcast(FP8X4), scales=plane,
+                                  in_=grouped[key][:].rearrange("p a r u -> p (a r u)").bitcast(BF16))
+
+        def quantize_y(i, g0, ng):
+            cols = slice(g0 * P, (g0 + ng) * P)
+            quantize(("y", i, g0), y_codes[i][:, cols], y_plane[i][:, cols])
+
+        def sort_x(j):
+            s = stage.tile([P, 2, K // 4], F32, name="x_sorted", align_bytes=64)
+            nc.vector.tensor_copy(out=s[:], in_=x_raw[j][:].bitcast(F32).rearrange("p (q u) -> p u q", u=2))
+            x_sorted[j] = s
+
+        def turn_x(pair):
+            for g in range(PASSES):
+                bank = turn_bank(g)
+                for a in range(2):
+                    for u in range(2):
+                        nc.tensor.transpose(bank[:, a, u, :], x_sorted[2 * pair + a][:, u, g * P:(g + 1) * P], ident[:])
+                turned["x", pair, g] = (bank, 2)
+
+        def quantize_x(pair, g):
+            cols = slice((pair % 2) * 2 * P, (pair % 2 + 1) * 2 * P)
+            quantize(("x", pair, g), x_codes[pair // 2, g][:, cols], x_plane[pair // 2, g][:, cols])
+
+        def product(kind, i, h, passes=range(PASSES), spare=False):
+            if spare:
+                sums[kind, i, h] = psum.tile([P, HALF], F32, name="bank3")
+            if (kind, i, h) not in sums:
+                name = "bank%d" % (4 + len(sum_count) % SUM_BANKS)
+                sum_count.append(name)
+                sums[kind, i, h] = psum.tile([P, HALF], F32, name=name)
+            for g in passes:
+                if kind == "a":
+                    rhs = a_codes[g][:, 2 * h * HALF:2 * (h + 1) * HALF].bitcast(FP4X4)
+                    scale = a_plane[g // 2][:, g % 2, h * HALF:(h + 1) * HALF]
+                elif kind == "b":
+                    rhs = b_codes[h, g // 2][:, g % 2, :].bitcast(FP8X4)
+                    scale = b_plane[4 * g:P, h * HALF:(h + 1) * HALF]
+                else:
+                    rhs, scale = x_codes[h, g][:].bitcast(FP8X4), x_plane[h, g][:]
+                cols = slice(g * P, (g + 1) * P)
+                nc.tensor.matmul_mx(out=sums[kind, i, h][:], lhsT=y_codes[i][:, cols].bitcast(FP8X4),
+                                    lhsT_scale=y_plane[i][:, cols], rhs=rhs, rhs_scale=scale,
+                                    start=(g == 0), stop=(g == PASSES - 1))
+
+        def empty(kind, i, h):
+            bank = sums[kind, i, h]
+            if kind == "a":
+                part = keep.tile([P, HALF], F32, name="partial%d_%d" % (i, h))
+                nc.scalar.copy(out=part[:], in_=bank[:])
+                partial[i, h] = part
+            else:
+                part = partial[i, h]
+                nc.vector.tensor_tensor(out=part[:], in0=bank[:], in1=part[:], op=ALU.mult if kind == "b" else ALU.add)
+                if kind == "x":
+                    nc.sync.dma_start(out=out[i * P:(i + 1) * P, h * HALF:(h + 1) * HALF], in_=part[:])
+
+        chunks = [(i, g, 1) for i in range(2) for g in range(PASSES)]
+        for step in range(len(chunks) + 3):
+            if 0 <= step - 3 < len(chunks):
+                copy_out(("y",) + chunks[step - 3][:2])
+            if step < len(chunks):
+                root(*chunks[step])
+            if 0 <= step - 1 < len(chunks):
+                power(*chunks[step - 1])
+                turn_y(*chunks[step - 1])
+            if 0 <= step - 3 < len(chunks):
+                quantize_y(*chunks[step - 3])
+                i, g0, ng = chunks[step - 3]
+                for g in range(g0, g0 + ng):
+                    product("a", i, 0, [g])
+                    product("a", i, 1, [g])
+
+        def make_y(i):
+            for c in (0, 2):
+                root(i, c, 2)
+            for c in (0, 2):
+                power(i, c, 2)
+
+        def turn_y_tile(i):
+            for c in (0, 2):
+                turn_y(i, c, 2)
+            for c in (0, 2):
+                copy_out(("y", i, c))
+
+        def quantize_y_tile(i):
+            for c in (0, 2):
+                quantize_y(i, c, 2)
+
+        def full(kind, i, h):
+            product(kind, i, h)
+            empty(kind, i, h)
+
+        root(2, 0, 2)
+        empty("a", 0, 0)
+        power(2, 0, 2)
+        product("b", 0, 0, [0, 1], spare=True)
+        product("b", 1, 0, [0, 1])
+        root(2, 2, 2)
+        empty("a", 0, 1)
+        empty("a", 1, 0)
+        power(2, 2, 2)
+        product("b", 0, 0, [2, 3])
+        product("b", 1, 0, [2, 3])
+        empty("a", 1, 1)
+        empty("b", 0, 0)
+        product("b", 0, 1, [0, 1])
+        turn_y_tile(2)
+        empty("b", 1, 0)
+        product("b", 1, 1, [0, 1])
+        product("b", 0, 1, [2, 3])
+        product("b", 1, 1, [2, 3])
+        quantize_y_tile(2)
+        root(3, 0, 2)
+        root(3, 2, 2)
+        empty("b", 0, 1)
+        empty("b", 1, 1)
+        power(3, 0, 2)
+        power(3, 2, 2)
+        full("a", 2, 0)
+        sort_x(0)
+        sort_x(1)
+        full("a", 2, 1)
+        turn_y_tile(3)
+        product("b", 2, 0)
+        quantize_y_tile(3)
+        empty("b", 2, 0)
+        rest = [("b", 2, 1), ("a", 3, 0), ("a", 3, 1), ("b", 3, 0), ("b", 3, 1), ("x", 0, 0), ("x", 1, 0), ("x", 2, 0)]
+        for pair in range(4):
+            turn_x(pair)
+            if pair < 3:
+                sort_x(2 * pair + 2)
+                sort_x(2 * pair + 3)
+            for g in range(PASSES):
+                copy_out(("x", pair, g))
+            first, second = rest[2 * pair:2 * pair + 2]
+            product(*first)
+            quantize_x(pair, 0)
+            quantize_x(pair, 1)
+            empty(*first)
+            product(*second)
+            quantize_x(pair, 2)
+            quantize_x(pair, 3)
+            empty(*second)
+        full("x", 3, 0)
+        for i in range(M_TILES - 1):
+            full("x", i, 1)
+        last = M_TILES - 1
+        for n0, width, index in ((0, 256, 0), (256, 128, 1), (384, 128, 2)):
+            bank = psum.tile([P, width], F32, name="bank%d" % index)
+            for g in range(PASSES):
+                cols = slice(g * P, (g + 1) * P)
+                nc.tensor.matmul_mx(out=bank[:], lhsT=y_codes[last][:, cols].bitcast(FP8X4),
+                                    lhsT_scale=y_plane[last][:, cols],
+                                    rhs=x_codes[1, g][:, n0:n0 + width].bitcast(FP8X4),
+                                    rhs_scale=x_plane[1, g][:, n0:n0 + width],
+                                    start=(g == 0), stop=(g == PASSES - 1))
+            part = partial[last, 1][:, n0:n0 + width]
+            nc.vector.tensor_tensor(out=part, in0=bank[:], in1=part, op=ALU.add)
+            nc.sync.dma_start(out=out[last * P:(last + 1) * P, HALF + n0:HALF + n0 + width], in_=part)

@@ -35,7 +35,6 @@ def tile_fractional_covariance_product_s10_kernel(tc, z, a_words, a_scales, b_wo
         ctx.enter_context(tc.manual_schedule())
 
         ident = keep.tile([P, P], F32, name="ident")
-        make_identity(nc, ident[:])
 
         a_plane = []
         for c in range(2):
@@ -45,6 +44,8 @@ def tile_fractional_covariance_product_s10_kernel(tc, z, a_words, a_scales, b_wo
         one = keep.tile([P, 8], F32, name="one")
         nc.vector.memset(one[:], 1.0)
         nc.vector.memset(a_plane[0][:].rearrange("p g n -> p (g n)").bitcast(I32), 0)
+        nc.vector.memset(ident[:], 0.0)
+        make_identity(nc, ident[:], nomemset=True)
         nc.vector.memset(a_plane[1][:].rearrange("p g n -> p (g n)").bitcast(I32), 0)
         nc.vector.memset(b_plane[:].bitcast(I32), 0)
         warm = keep.tile([P, 8], F32, name="warm")
@@ -130,9 +131,13 @@ def tile_fractional_covariance_product_s10_kernel(tc, z, a_words, a_scales, b_wo
             raw, first = z_raw[i, g0]
             return raw[:, first * 512:(first + ng) * 512].rearrange("p (q u e) -> p u q e", u=2, e=2)
 
-        def root(i, g0, ng):
+        def root(i, g0, ng, split=False):
             r = stage.tile([P, 2, ng * P, 2], F32, name="root", align_bytes=64)
-            nc.scalar.activation(out=r[:], in_=z_view(i, g0, ng), func=ACT.Abs_reciprocal_sqrt)
+            if split:
+                for u in range(2):
+                    nc.scalar.activation(out=r[:, u], in_=z_view(i, g0, ng)[:, u], func=ACT.Abs_reciprocal_sqrt)
+            else:
+                nc.scalar.activation(out=r[:], in_=z_view(i, g0, ng), func=ACT.Abs_reciprocal_sqrt)
             roots[i, g0] = r
 
         def power(i, g0, ng):
@@ -143,8 +148,7 @@ def tile_fractional_covariance_product_s10_kernel(tc, z, a_words, a_scales, b_wo
             y_sorted[i, g0] = y
 
         def turn_y(i, g0, ng):
-            bank = turn_bank(len(turn_count) % 3)
-            turn_count.append(bank)
+            bank = turn_bank(g0)
             words = y_sorted[i, g0][:].rearrange("p u q e -> p u (q e)").bitcast(F32)
             for g in range(ng):
                 for u in range(2):
@@ -215,22 +219,59 @@ def tile_fractional_covariance_product_s10_kernel(tc, z, a_words, a_scales, b_wo
                 if kind == "x":
                     nc.sync.dma_start(out=out[i * P:(i + 1) * P, h * HALF:(h + 1) * HALF], in_=part[:])
 
-        chunks = [(i, g, 1) for i in range(2) for g in range(PASSES)]
-        for step in range(len(chunks) + 3):
-            if 0 <= step - 3 < len(chunks):
-                copy_out(("y",) + chunks[step - 3][:2])
-            if step < len(chunks):
-                root(*chunks[step])
-            if 0 <= step - 1 < len(chunks):
-                power(*chunks[step - 1])
-                turn_y(*chunks[step - 1])
-            if 0 <= step - 3 < len(chunks):
-                quantize_y(*chunks[step - 3])
-                i, g0, ng = chunks[step - 3]
-                for g in range(g0, g0 + ng):
-                    product("a", i, 0, [g])
-                    product("a", i, 1, [g])
+        def a_passes(i, passes):
+            for g in passes:
+                product("a", i, 0, [g])
+                product("a", i, 1, [g])
 
+        root(0, 0, 1, split=True)
+        power(0, 0, 1)
+        root(0, 1, 1)
+        turn_y(0, 0, 1)
+        power(0, 1, 1)
+        root(0, 2, 1)
+        turn_y(0, 1, 1)
+        copy_out(("y", 0, 0))
+        quantize_y(0, 0, 1)
+        a_passes(0, range(0, 1))
+        root(0, 3, 1)
+        power(0, 2, 1)
+        copy_out(("y", 0, 1))
+        quantize_y(0, 1, 1)
+        power(0, 3, 1)
+        turn_y(0, 2, 1)
+        turn_y(0, 3, 1)
+        a_passes(0, range(1, 2))
+        root(1, 0, 1)
+        power(1, 0, 1)
+        root(1, 1, 1)
+        copy_out(("y", 0, 2))
+        copy_out(("y", 0, 3))
+        power(1, 1, 1)
+        quantize_y(0, 2, 1)
+        quantize_y(0, 3, 1)
+        turn_y(1, 0, 1)
+        turn_y(1, 1, 1)
+        a_passes(0, range(2, 3))
+        a_passes(0, range(3, 4))
+        root(1, 2, 1)
+        power(1, 2, 1)
+        root(1, 3, 1)
+        copy_out(("y", 1, 0))
+        copy_out(("y", 1, 1))
+        power(1, 3, 1)
+        quantize_y(1, 0, 1)
+        quantize_y(1, 1, 1)
+        turn_y(1, 2, 1)
+        turn_y(1, 3, 1)
+        a_passes(1, range(0, 1))
+        a_passes(1, range(1, 2))
+        copy_out(("y", 1, 2))
+        copy_out(("y", 1, 3))
+        quantize_y(1, 2, 1)
+        quantize_y(1, 3, 1)
+        a_passes(1, range(2, 3))
+        a_passes(1, range(3, 4))
         def make_y(i):
             for c in (0, 2):
                 root(i, c, 2)
@@ -279,13 +320,14 @@ def tile_fractional_covariance_product_s10_kernel(tc, z, a_words, a_scales, b_wo
         power(3, 2, 2)
         full("a", 2, 0)
         sort_x(0)
-        sort_x(1)
         full("a", 2, 1)
+        sort_x(1)
+        full("b", 2, 0)
         turn_y_tile(3)
-        product("b", 2, 0)
+        product("b", 2, 1)
         quantize_y_tile(3)
-        empty("b", 2, 0)
-        rest = [("b", 2, 1), ("a", 3, 0), ("a", 3, 1), ("b", 3, 0), ("b", 3, 1), ("x", 0, 0), ("x", 1, 0), ("x", 2, 0)]
+        empty("b", 2, 1)
+        rest = [("a", 3, 0), ("a", 3, 1), ("b", 3, 0), ("b", 3, 1), ("x", 0, 0), ("x", 1, 0), ("x", 2, 0), ("x", 3, 0)]
         for pair in range(4):
             turn_x(pair)
             if pair < 3:
@@ -302,19 +344,18 @@ def tile_fractional_covariance_product_s10_kernel(tc, z, a_words, a_scales, b_wo
             quantize_x(pair, 2)
             quantize_x(pair, 3)
             empty(*second)
-        full("x", 3, 0)
-        for i in range(M_TILES - 1):
+        pieces = [(2, 0, 256), (2, 256, 256), (3, 0, 256), (3, 256, 128), (3, 384, 128)]
+        for i in range(pieces[0][0]):
             full("x", i, 1)
-        last = M_TILES - 1
-        for n0, width, index in ((0, 256, 0), (256, 128, 1), (384, 128, 2)):
+        for index, (i, n0, width) in enumerate(pieces):
             bank = psum.tile([P, width], F32, name="bank%d" % index)
             for g in range(PASSES):
                 cols = slice(g * P, (g + 1) * P)
-                nc.tensor.matmul_mx(out=bank[:], lhsT=y_codes[last][:, cols].bitcast(FP8X4),
-                                    lhsT_scale=y_plane[last][:, cols],
+                nc.tensor.matmul_mx(out=bank[:], lhsT=y_codes[i][:, cols].bitcast(FP8X4),
+                                    lhsT_scale=y_plane[i][:, cols],
                                     rhs=x_codes[1, g][:, n0:n0 + width].bitcast(FP8X4),
                                     rhs_scale=x_plane[1, g][:, n0:n0 + width],
                                     start=(g == 0), stop=(g == PASSES - 1))
-            part = partial[last, 1][:, n0:n0 + width]
+            part = partial[i, 1][:, n0:n0 + width]
             nc.vector.tensor_tensor(out=part, in0=bank[:], in1=part, op=ALU.add)
-            nc.sync.dma_start(out=out[last * P:(last + 1) * P, HALF + n0:HALF + n0 + width], in_=part)
+            nc.sync.dma_start(out=out[i * P:(i + 1) * P, HALF + n0:HALF + n0 + width], in_=part)

@@ -17,13 +17,15 @@ ALU = mybir.AluOpType
 ACT = mybir.ActivationFunctionType
 
 P = 128
-PASSES = K // 512
+K_PASS = 4 * P
+PASSES = K // K_PASS
 HALF = 512
-M_TILES = M // P
+Y_TILES = M // P
 X_TILES = N // P
+BANKS = 8
 TURN_BANKS = 4
-SUM_BANKS = 4
-FINITE = 2.0 ** 100
+ROOT_CAP = 2.0 ** 67
+LAST_PIECES = [(2, 0, 256), (2, 256, 256), (3, 0, 256), (3, 256, 128), (3, 384, 128)]
 
 
 def tile_fractional_covariance_product_s10_kernel(tc, z, a_words, a_scales, b_words, b_scales, x, out):
@@ -34,29 +36,21 @@ def tile_fractional_covariance_product_s10_kernel(tc, z, a_words, a_scales, b_wo
         psum = ctx.enter_context(tc.psum_pool(name="psum", bufs=1))
         ctx.enter_context(tc.manual_schedule())
 
+        a_scale = [keep.tile([P, 2, N], U8, name="a_scale%d" % c, align_bytes=64) for c in range(2)]
+        b_scale = keep.tile([P, N], U8, name="b_scale", align_bytes=64)
         ident = keep.tile([P, P], F32, name="ident")
-
-        a_plane = []
-        for c in range(2):
-            plane = keep.tile([P, 2, N], U8, name="a_plane%d" % c, align_bytes=64)
-            a_plane.append(plane)
-        b_plane = keep.tile([P, N], U8, name="b_plane", align_bytes=64)
-        one = keep.tile([P, 8], F32, name="one")
-        nc.vector.memset(one[:], 1.0)
-        nc.vector.memset(a_plane[0][:].rearrange("p g n -> p (g n)").bitcast(I32), 0)
+        nc.vector.memset(a_scale[0][:].rearrange("p g n -> p (g n)").bitcast(I32), 0)
         nc.vector.memset(ident[:], 0.0)
         make_identity(nc, ident[:], nomemset=True)
-        nc.vector.memset(a_plane[1][:].rearrange("p g n -> p (g n)").bitcast(I32), 0)
-        nc.vector.memset(b_plane[:].bitcast(I32), 0)
-        warm = keep.tile([P, 8], F32, name="warm")
-        nc.scalar.activation(out=warm[:], in_=one[:], func=ACT.Abs_reciprocal_sqrt)
+        nc.vector.memset(a_scale[1][:].rearrange("p g n -> p (g n)").bitcast(I32), 0)
+        nc.vector.memset(b_scale[:].bitcast(I32), 0)
 
         z_raw, x_raw, a_codes, b_codes = {}, {}, {}, {}
 
-        def load_z(i, g0, ng):
-            raw = keep.tile([P, ng * 512], BF16, name="z%d_%d" % (i, g0), align_bytes=64)
-            nc.sync.dma_start(out=raw[:], in_=z[i * P:(i + 1) * P, g0 * 512:(g0 + ng) * 512])
-            for g in range(ng):
+        def load_z(i, g0, passes):
+            raw = keep.tile([P, passes * K_PASS], BF16, name="z%d_%d" % (i, g0), align_bytes=64)
+            nc.sync.dma_start(out=raw[:], in_=z[i * P:(i + 1) * P, g0 * K_PASS:(g0 + passes) * K_PASS])
+            for g in range(passes):
                 z_raw[i, g0 + g] = (raw, g)
 
         def load_x(j):
@@ -67,7 +61,7 @@ def tile_fractional_covariance_product_s10_kernel(tc, z, a_words, a_scales, b_wo
         def load_a_scales(c):
             rows = a_scales.rearrange("g (q r) n -> r q g n", r=4)
             for r in range(4):
-                nc.sync.dma_start(out=a_plane[c][r:P:32, :, :].bitcast(I32),
+                nc.sync.dma_start(out=a_scale[c][r:P:32, :, :].bitcast(I32),
                                   in_=rows[r][:, 2 * c:2 * c + 2, :].bitcast(I32))
 
         def load_a(g):
@@ -77,7 +71,7 @@ def tile_fractional_covariance_product_s10_kernel(tc, z, a_words, a_scales, b_wo
 
         def load_b_scales():
             for q in range(4):
-                nc.sync.dma_start(out=b_plane[32 * q:32 * q + 16, :].bitcast(I32),
+                nc.sync.dma_start(out=b_scale[32 * q:32 * q + 16, :].bitcast(I32),
                                   in_=b_scales[:, 4 * q:4 * q + 4, :].bitcast(I32))
 
         def load_b(h):
@@ -99,263 +93,233 @@ def tile_fractional_covariance_product_s10_kernel(tc, z, a_words, a_scales, b_wo
         load_a(2)
         load_z(1, 2, 2)
         load_a(3)
-        load_z(2, 0, 4)
+        load_z(2, 0, PASSES)
         load_b_scales()
         load_b(0)
         load_b(1)
-        load_z(3, 0, 4)
+        load_z(3, 0, PASSES)
         for j in range(X_TILES):
             load_x(j)
 
-        y_codes, y_plane = [], []
-        for i in range(M_TILES):
-            codes = keep.tile([P, PASSES * P], U32, name="y_codes%d" % i, align_bytes=64)
-            plane = keep.tile([P, PASSES * P], U8, name="y_plane%d" % i, align_bytes=64)
-            y_codes.append(codes)
-            y_plane.append(plane)
-        x_codes, x_plane = {}, {}
+        y_codes = [keep.tile([P, PASSES * P], U32, name="y_codes%d" % i, align_bytes=64) for i in range(Y_TILES)]
+        y_scale = [keep.tile([P, PASSES * P], U8, name="y_scale%d" % i, align_bytes=64) for i in range(Y_TILES)]
+        x_codes, x_scale = {}, {}
         for h in range(2):
             for g in range(PASSES):
-                codes = keep.tile([P, HALF], U32, name="x_codes%d_%d" % (h, g), align_bytes=64)
-                plane = keep.tile([P, HALF], U8, name="x_plane%d_%d" % (h, g), align_bytes=64)
-                x_codes[h, g] = codes
-                x_plane[h, g] = plane
+                x_codes[h, g] = keep.tile([P, HALF], U32, name="x_codes%d_%d" % (h, g), align_bytes=64)
+                x_scale[h, g] = keep.tile([P, HALF], U8, name="x_scale%d_%d" % (h, g), align_bytes=64)
 
-        turn_count, sum_count = [], []
         roots, y_sorted, x_sorted, turned, grouped, sums, partial = {}, {}, {}, {}, {}, {}, {}
 
-        def turn_bank(index):
-            return psum.tile([P, 2, 2, P], F32, name="bank%d" % index)
+        def bank_tile(shape, bank):
+            return psum.tile(shape, F32, name="bank%d" % bank)
 
-        def z_view(i, g0, ng):
+        def z_by_parity(i, g0, passes):
             raw, first = z_raw[i, g0]
-            return raw[:, first * 512:(first + ng) * 512].rearrange("p (q u e) -> p u q e", u=2, e=2)
+            return raw[:, first * K_PASS:(first + passes) * K_PASS].rearrange("p (w u e) -> p u w e", u=2, e=2)
 
-        def root(i, g0, ng, split=False):
-            r = stage.tile([P, 2, ng * P, 2], F32, name="root", align_bytes=64)
-            if split:
-                for u in range(2):
-                    nc.scalar.activation(out=r[:, u], in_=z_view(i, g0, ng)[:, u], func=ACT.Abs_reciprocal_sqrt)
-            else:
-                nc.scalar.activation(out=r[:], in_=z_view(i, g0, ng), func=ACT.Abs_reciprocal_sqrt)
-            roots[i, g0] = r
+        def root(i, g0, passes, parities=(slice(0, 2),)):
+            inverse = stage.tile([P, 2, passes * P, 2], F32, name="root", align_bytes=64)
+            for u in parities:
+                nc.scalar.activation(out=inverse[:, u], in_=z_by_parity(i, g0, passes)[:, u],
+                                     func=ACT.Abs_reciprocal_sqrt)
+            roots[i, g0] = inverse
 
-        def power(i, g0, ng):
-            y = stage.tile([P, 2, ng * P, 2], BF16, name="y_sorted", align_bytes=64)
+        def power(i, g0, passes):
+            y = stage.tile([P, 2, passes * P, 2], BF16, name="y_sorted", align_bytes=64)
             for u in range(2):
-                nc.vector.scalar_tensor_tensor(out=y[:, u], in0=roots[i, g0][:, u], scalar=FINITE,
-                                               in1=z_view(i, g0, ng)[:, u], op0=ALU.min, op1=ALU.mult)
+                nc.vector.scalar_tensor_tensor(out=y[:, u], in0=roots[i, g0][:, u], scalar=ROOT_CAP,
+                                               in1=z_by_parity(i, g0, passes)[:, u], op0=ALU.min, op1=ALU.mult)
             y_sorted[i, g0] = y
 
-        def turn_y(i, g0, ng):
-            bank = turn_bank(g0)
-            words = y_sorted[i, g0][:].rearrange("p u q e -> p u (q e)").bitcast(F32)
-            for g in range(ng):
-                for u in range(2):
-                    nc.tensor.transpose(bank[:, g, u, :], words[:, u, g * P:(g + 1) * P], ident[:])
-            turned["y", i, g0] = (bank, ng)
-
-        def copy_out(key):
-            bank, count = turned[key]
-            tile = stage.tile([P, count, P, 2], F32, name="grouped", bufs=6, align_bytes=64)
-            nc.scalar.copy(out=tile[:], in_=bank[:, 0:count].rearrange("p a u r -> p a r u"))
-            grouped[key] = tile
-
-        def quantize(key, codes, plane):
-            nc.vector.quantize_mx(out=codes.bitcast(FP8X4), scales=plane,
-                                  in_=grouped[key][:].rearrange("p a r u -> p (a r u)").bitcast(BF16))
-
-        def quantize_y(i, g0, ng):
-            cols = slice(g0 * P, (g0 + ng) * P)
-            quantize(("y", i, g0), y_codes[i][:, cols], y_plane[i][:, cols])
-
         def sort_x(j):
-            s = stage.tile([P, 2, K // 4], F32, name="x_sorted", align_bytes=64)
-            nc.vector.tensor_copy(out=s[:], in_=x_raw[j][:].bitcast(F32).rearrange("p (q u) -> p u q", u=2))
-            x_sorted[j] = s
+            pairs = stage.tile([P, 2, PASSES * P], F32, name="x_sorted", align_bytes=64)
+            nc.vector.tensor_copy(out=pairs[:], in_=x_raw[j][:].bitcast(F32).rearrange("p (w u) -> p u w", u=2))
+            x_sorted[j] = pairs
 
-        def turn_x(pair):
-            for g in range(PASSES):
-                bank = turn_bank(g)
-                for a in range(2):
-                    for u in range(2):
-                        nc.tensor.transpose(bank[:, a, u, :], x_sorted[2 * pair + a][:, u, g * P:(g + 1) * P], ident[:])
-                turned["x", pair, g] = (bank, 2)
+        def turn(unit, bank):
+            if unit[0] == "y":
+                i, g0, passes = unit[1:]
+                pairs = y_sorted[i, g0][:].rearrange("p u w e -> p u (w e)").bitcast(F32)
+                blocks = [pairs[:, :, g * P:(g + 1) * P] for g in range(passes)]
+            else:
+                d, g = unit[1:]
+                blocks = [x_sorted[j][:, :, g * P:(g + 1) * P] for j in (2 * d, 2 * d + 1)]
+            tile = bank_tile([P, 2, 2, P], bank)
+            for a, block in enumerate(blocks):
+                for u in range(2):
+                    nc.tensor.transpose(tile[:, a, u, :], block[:, u, :], ident[:])
+            turned[unit] = (tile, len(blocks))
 
-        def quantize_x(pair, g):
-            cols = slice((pair % 2) * 2 * P, (pair % 2 + 1) * 2 * P)
-            quantize(("x", pair, g), x_codes[pair // 2, g][:, cols], x_plane[pair // 2, g][:, cols])
+        def copy_out(unit):
+            tile, count = turned[unit]
+            pairs = stage.tile([P, count, P, 2], F32, name="grouped", bufs=6, align_bytes=64)
+            nc.scalar.copy(out=pairs[:], in_=tile[:, 0:count].rearrange("p a u r -> p a r u"))
+            grouped[unit] = pairs
 
-        def product(kind, i, h, passes=range(PASSES), spare=False):
-            if spare:
-                sums[kind, i, h] = psum.tile([P, HALF], F32, name="bank3")
-            if (kind, i, h) not in sums:
-                name = "bank%d" % (4 + len(sum_count) % SUM_BANKS)
-                sum_count.append(name)
-                sums[kind, i, h] = psum.tile([P, HALF], F32, name=name)
+        def quantize(unit):
+            if unit[0] == "y":
+                i, g0, passes = unit[1:]
+                cols = slice(g0 * P, (g0 + passes) * P)
+                codes, scale = y_codes[i], y_scale[i]
+            else:
+                d, g = unit[1:]
+                cols = slice(d % 2 * 2 * P, (d % 2 + 1) * 2 * P)
+                codes, scale = x_codes[d // 2, g], x_scale[d // 2, g]
+            nc.vector.quantize_mx(out=codes[:, cols].bitcast(FP8X4), scales=scale[:, cols],
+                                  in_=grouped[unit][:].rearrange("p a r u -> p (a r u)").bitcast(BF16))
+
+        def multiply(acc, kind, i, h, passes, cols):
             for g in passes:
                 if kind == "a":
-                    rhs = a_codes[g][:, 2 * h * HALF:2 * (h + 1) * HALF].bitcast(FP4X4)
-                    scale = a_plane[g // 2][:, g % 2, h * HALF:(h + 1) * HALF]
+                    codes = a_codes[g][:, 2 * h * HALF:2 * (h + 1) * HALF].bitcast(FP4X4)
+                    scale = a_scale[g // 2][:, g % 2, h * HALF:(h + 1) * HALF]
                 elif kind == "b":
-                    rhs = b_codes[h, g // 2][:, g % 2, :].bitcast(FP8X4)
-                    scale = b_plane[4 * g:P, h * HALF:(h + 1) * HALF]
+                    codes = b_codes[h, g // 2][:, g % 2, :].bitcast(FP8X4)
+                    scale = b_scale[4 * g:P, h * HALF:(h + 1) * HALF]
                 else:
-                    rhs, scale = x_codes[h, g][:].bitcast(FP8X4), x_plane[h, g][:]
-                cols = slice(g * P, (g + 1) * P)
-                nc.tensor.matmul_mx(out=sums[kind, i, h][:], lhsT=y_codes[i][:, cols].bitcast(FP8X4),
-                                    lhsT_scale=y_plane[i][:, cols], rhs=rhs, rhs_scale=scale,
+                    codes, scale = x_codes[h, g][:, cols].bitcast(FP8X4), x_scale[h, g][:, cols]
+                y_cols = slice(g * P, (g + 1) * P)
+                nc.tensor.matmul_mx(out=acc, lhsT=y_codes[i][:, y_cols].bitcast(FP8X4),
+                                    lhsT_scale=y_scale[i][:, y_cols], rhs=codes, rhs_scale=scale,
                                     start=(g == 0), stop=(g == PASSES - 1))
 
-        def empty(kind, i, h):
-            bank = sums[kind, i, h]
+        def product(group, bank, passes=range(PASSES)):
+            if group not in sums:
+                sums[group] = bank_tile([P, HALF], bank)
+            multiply(sums[group][:], *group, passes, slice(0, HALF))
+
+        def add_and_store(acc, i, h, cols):
+            part = partial[i, h][:, cols]
+            nc.vector.tensor_tensor(out=part, in0=acc, in1=part, op=ALU.add)
+            nc.sync.dma_start(out=out[i * P:(i + 1) * P, h * HALF + cols.start:h * HALF + cols.stop], in_=part)
+
+        def empty(group):
+            kind, i, h = group
             if kind == "a":
-                part = keep.tile([P, HALF], F32, name="partial%d_%d" % (i, h))
-                nc.scalar.copy(out=part[:], in_=bank[:])
-                partial[i, h] = part
+                partial[i, h] = keep.tile([P, HALF], F32, name="partial%d_%d" % (i, h))
+                nc.scalar.copy(out=partial[i, h][:], in_=sums[group][:])
+            elif kind == "b":
+                nc.vector.tensor_tensor(out=partial[i, h][:], in0=sums[group][:], in1=partial[i, h][:], op=ALU.mult)
             else:
-                part = partial[i, h]
-                nc.vector.tensor_tensor(out=part[:], in0=bank[:], in1=part[:], op=ALU.mult if kind == "b" else ALU.add)
-                if kind == "x":
-                    nc.sync.dma_start(out=out[i * P:(i + 1) * P, h * HALF:(h + 1) * HALF], in_=part[:])
+                add_and_store(sums[group][:], i, h, slice(0, HALF))
 
-        def a_passes(i, passes):
-            for g in passes:
-                product("a", i, 0, [g])
-                product("a", i, 1, [g])
+        def a_passes(i, g):
+            for h in range(2):
+                product(("a", i, h), TURN_BANKS + 2 * i + h, [g])
 
-        root(0, 0, 1, split=True)
-        power(0, 0, 1)
-        root(0, 1, 1)
-        turn_y(0, 0, 1)
-        power(0, 1, 1)
-        root(0, 2, 1)
-        turn_y(0, 1, 1)
-        copy_out(("y", 0, 0))
-        quantize_y(0, 0, 1)
-        a_passes(0, range(0, 1))
-        root(0, 3, 1)
-        power(0, 2, 1)
-        copy_out(("y", 0, 1))
-        quantize_y(0, 1, 1)
-        power(0, 3, 1)
-        turn_y(0, 2, 1)
-        turn_y(0, 3, 1)
-        a_passes(0, range(1, 2))
-        root(1, 0, 1)
-        power(1, 0, 1)
-        root(1, 1, 1)
-        copy_out(("y", 0, 2))
-        copy_out(("y", 0, 3))
-        power(1, 1, 1)
-        quantize_y(0, 2, 1)
-        quantize_y(0, 3, 1)
-        turn_y(1, 0, 1)
-        turn_y(1, 1, 1)
-        a_passes(0, range(2, 3))
-        a_passes(0, range(3, 4))
-        root(1, 2, 1)
-        power(1, 2, 1)
-        root(1, 3, 1)
-        copy_out(("y", 1, 0))
-        copy_out(("y", 1, 1))
-        power(1, 3, 1)
-        quantize_y(1, 0, 1)
-        quantize_y(1, 1, 1)
-        turn_y(1, 2, 1)
-        turn_y(1, 3, 1)
-        a_passes(1, range(0, 1))
-        a_passes(1, range(1, 2))
-        copy_out(("y", 1, 2))
-        copy_out(("y", 1, 3))
-        quantize_y(1, 2, 1)
-        quantize_y(1, 3, 1)
-        a_passes(1, range(2, 3))
-        a_passes(1, range(3, 4))
-        def make_y(i):
-            for c in (0, 2):
-                root(i, c, 2)
-            for c in (0, 2):
-                power(i, c, 2)
+        single = [(i, g, 1) for i in range(2) for g in range(PASSES)]
+        units = [("y",) + chunk for chunk in single]
+        root(*single[0], parities=(slice(0, 1), slice(1, 2)))
+        power(*single[0])
+        root(*single[1])
+        turn(units[0], 0)
+        power(*single[1])
+        root(*single[2])
+        turn(units[1], 1)
+        copy_out(units[0])
+        quantize(units[0])
+        a_passes(0, 0)
+        root(*single[3])
+        power(*single[2])
+        copy_out(units[1])
+        quantize(units[1])
+        power(*single[3])
+        turn(units[2], 2)
+        turn(units[3], 3)
+        a_passes(0, 1)
+        for n in range(4, len(single) + 1, 2):
+            new, old = range(n, min(n + 2, len(single))), (n - 2, n - 1)
+            for idx in new[:1]:
+                root(*single[idx])
+                power(*single[idx])
+                root(*single[idx + 1])
+            for idx in old:
+                copy_out(units[idx])
+            for idx in new[1:]:
+                power(*single[idx])
+            for idx in old:
+                quantize(units[idx])
+            for idx in new:
+                turn(units[idx], single[idx][1])
+            for idx in old:
+                a_passes(*single[idx][:2])
 
-        def turn_y_tile(i):
-            for c in (0, 2):
-                turn_y(i, c, 2)
-            for c in (0, 2):
-                copy_out(("y", i, c))
-
-        def quantize_y_tile(i):
-            for c in (0, 2):
-                quantize_y(i, c, 2)
-
-        def full(kind, i, h):
-            product(kind, i, h)
-            empty(kind, i, h)
-
+        early, late = range(0, 2), range(2, PASSES)
+        y2_units = [("y", 2, 0, 2), ("y", 2, 2, 2)]
         root(2, 0, 2)
-        empty("a", 0, 0)
+        empty(("a", 0, 0))
         power(2, 0, 2)
-        product("b", 0, 0, [0, 1], spare=True)
-        product("b", 1, 0, [0, 1])
+        product(("b", 0, 0), 3, early)
+        product(("b", 1, 0), 4, early)
         root(2, 2, 2)
-        empty("a", 0, 1)
-        empty("a", 1, 0)
+        empty(("a", 0, 1))
+        empty(("a", 1, 0))
         power(2, 2, 2)
-        product("b", 0, 0, [2, 3])
-        product("b", 1, 0, [2, 3])
-        empty("a", 1, 1)
-        empty("b", 0, 0)
-        product("b", 0, 1, [0, 1])
-        turn_y_tile(2)
-        empty("b", 1, 0)
-        product("b", 1, 1, [0, 1])
-        product("b", 0, 1, [2, 3])
-        product("b", 1, 1, [2, 3])
-        quantize_y_tile(2)
+        product(("b", 0, 0), 3, late)
+        product(("b", 1, 0), 4, late)
+        empty(("a", 1, 1))
+        empty(("b", 0, 0))
+        product(("b", 0, 1), 5, early)
+        for unit in y2_units:
+            turn(unit, unit[2])
+        for unit in y2_units:
+            copy_out(unit)
+        empty(("b", 1, 0))
+        product(("b", 1, 1), 6, early)
+        product(("b", 0, 1), 5, late)
+        product(("b", 1, 1), 6, late)
+        for unit in y2_units:
+            quantize(unit)
         root(3, 0, 2)
         root(3, 2, 2)
-        empty("b", 0, 1)
-        empty("b", 1, 1)
+        empty(("b", 0, 1))
+        empty(("b", 1, 1))
         power(3, 0, 2)
         power(3, 2, 2)
-        full("a", 2, 0)
-        sort_x(0)
-        full("a", 2, 1)
-        sort_x(1)
-        full("b", 2, 0)
-        turn_y_tile(3)
-        product("b", 2, 1)
-        quantize_y_tile(3)
-        empty("b", 2, 1)
-        rest = [("a", 3, 0), ("a", 3, 1), ("b", 3, 0), ("b", 3, 1), ("x", 0, 0), ("x", 1, 0), ("x", 2, 0), ("x", 3, 0)]
-        for pair in range(4):
-            turn_x(pair)
-            if pair < 3:
-                sort_x(2 * pair + 2)
-                sort_x(2 * pair + 3)
-            for g in range(PASSES):
-                copy_out(("x", pair, g))
-            first, second = rest[2 * pair:2 * pair + 2]
-            product(*first)
-            quantize_x(pair, 0)
-            quantize_x(pair, 1)
-            empty(*first)
-            product(*second)
-            quantize_x(pair, 2)
-            quantize_x(pair, 3)
-            empty(*second)
-        pieces = [(2, 0, 256), (2, 256, 256), (3, 0, 256), (3, 256, 128), (3, 384, 128)]
-        for i in range(pieces[0][0]):
-            full("x", i, 1)
-        for index, (i, n0, width) in enumerate(pieces):
-            bank = psum.tile([P, width], F32, name="bank%d" % index)
-            for g in range(PASSES):
-                cols = slice(g * P, (g + 1) * P)
-                nc.tensor.matmul_mx(out=bank[:], lhsT=y_codes[i][:, cols].bitcast(FP8X4),
-                                    lhsT_scale=y_plane[i][:, cols],
-                                    rhs=x_codes[1, g][:, n0:n0 + width].bitcast(FP8X4),
-                                    rhs_scale=x_plane[1, g][:, n0:n0 + width],
-                                    start=(g == 0), stop=(g == PASSES - 1))
-            part = partial[i, 1][:, n0:n0 + width]
-            nc.vector.tensor_tensor(out=part, in0=bank[:], in1=part, op=ALU.add)
-            nc.sync.dma_start(out=out[i * P:(i + 1) * P, HALF + n0:HALF + n0 + width], in_=part)
+
+        taken = []
+
+        def next_bank():
+            taken.append(TURN_BANKS + (len(taken) - 1) % (BANKS - TURN_BANKS))
+            return taken[-1]
+
+        y3_units = [("y", 3, 0, 2), ("y", 3, 2, 2)]
+        for h in range(2):
+            product(("a", 2, h), next_bank())
+            empty(("a", 2, h))
+            sort_x(h)
+        product(("b", 2, 0), next_bank())
+        empty(("b", 2, 0))
+        for unit in y3_units:
+            turn(unit, unit[2])
+        for unit in y3_units:
+            copy_out(unit)
+        product(("b", 2, 1), next_bank())
+        for unit in y3_units:
+            quantize(unit)
+        empty(("b", 2, 1))
+
+        groups = [(kind, 3, h) for kind in ("a", "b") for h in range(2)] + [("x", i, 0) for i in range(Y_TILES)]
+        for d in range(X_TILES // 2):
+            x_units = [("x", d, g) for g in range(PASSES)]
+            for unit in x_units:
+                turn(unit, unit[2])
+            for j in range(2 * d + 2, min(2 * d + 4, X_TILES)):
+                sort_x(j)
+            for unit in x_units:
+                copy_out(unit)
+            for step in range(2):
+                product(groups[2 * d + step], next_bank())
+                for unit in x_units[2 * step:2 * step + 2]:
+                    quantize(unit)
+                empty(groups[2 * d + step])
+
+        for i in range(LAST_PIECES[0][0]):
+            product(("x", i, 1), next_bank())
+            empty(("x", i, 1))
+        for bank, (i, n0, width) in enumerate(LAST_PIECES):
+            cols = slice(n0, n0 + width)
+            acc = bank_tile([P, width], bank)
+            multiply(acc[:], "x", i, 1, range(PASSES), cols)
+            add_and_store(acc[:], i, 1, cols)

from contextlib import ExitStack

import concourse.mybir as mybir
from concourse.masks import make_identity

M, K, N = 512, 2048, 1024
FLOPS = 3 * 2 * M * K * N

F32 = mybir.dt.float32
BF16 = mybir.dt.bfloat16
I32 = mybir.dt.int32
U32 = mybir.dt.uint32
U8 = mybir.dt.uint8
FP8X4 = mybir.dt.float8_e4m3fn_x4
FP4X4 = mybir.dt.float4_e2m1fn_x4
ALU = mybir.AluOpType
ACT = mybir.ActivationFunctionType

P = 128
K_PASS = 4 * P
PASSES = K // K_PASS
HALF = 512
Y_TILES = M // P
X_TILES = N // P
BANKS = 8
TURN_BANKS = 4
ROOT_CAP = 2.0 ** 67
LAST_PIECES = [(2, 0, 256), (2, 256, 256), (3, 0, 256), (3, 256, 128), (3, 384, 128)]


def tile_fractional_covariance_product_s10_kernel(tc, z, a_words, a_scales, b_words, b_scales, x, out):
    nc = tc.nc
    with ExitStack() as ctx:
        keep = ctx.enter_context(tc.tile_pool(name="keep", bufs=1))
        stage = ctx.enter_context(tc.tile_pool(name="stage", bufs=4))
        psum = ctx.enter_context(tc.psum_pool(name="psum", bufs=1))
        ctx.enter_context(tc.manual_schedule())

        a_scale = [keep.tile([P, 2, N], U8, name="a_scale%d" % c, align_bytes=64) for c in range(2)]
        b_scale = keep.tile([P, N], U8, name="b_scale", align_bytes=64)
        ident = keep.tile([P, P], F32, name="ident")
        nc.vector.memset(a_scale[0][:].rearrange("p g n -> p (g n)").bitcast(I32), 0)
        nc.vector.memset(ident[:], 0.0)
        make_identity(nc, ident[:], nomemset=True)
        nc.vector.memset(a_scale[1][:].rearrange("p g n -> p (g n)").bitcast(I32), 0)
        nc.vector.memset(b_scale[:].bitcast(I32), 0)

        z_raw, x_raw, a_codes, b_codes = {}, {}, {}, {}

        def load_z(i, g0, passes):
            raw = keep.tile([P, passes * K_PASS], BF16, name="z%d_%d" % (i, g0), align_bytes=64)
            nc.sync.dma_start(out=raw[:], in_=z[i * P:(i + 1) * P, g0 * K_PASS:(g0 + passes) * K_PASS])
            for g in range(passes):
                z_raw[i, g0 + g] = (raw, g)

        def load_x(j):
            raw = keep.tile([P, K], BF16, name="x%d" % j, align_bytes=64)
            nc.sync.dma_start(out=raw[:], in_=x[j * P:(j + 1) * P, :])
            x_raw[j] = raw

        def load_a_scales(c):
            rows = a_scales.rearrange("g (q r) n -> r q g n", r=4)
            for r in range(4):
                nc.sync.dma_start(out=a_scale[c][r:P:32, :, :].bitcast(I32),
                                  in_=rows[r][:, 2 * c:2 * c + 2, :].bitcast(I32))

        def load_a(g):
            codes = keep.tile([P, 2 * N], U8, name="a_codes%d" % g, align_bytes=64)
            nc.sync.dma_start(out=codes[:].bitcast(I32), in_=a_words[g].bitcast(I32))
            a_codes[g] = codes

        def load_b_scales():
            for q in range(4):
                nc.sync.dma_start(out=b_scale[32 * q:32 * q + 16, :].bitcast(I32),
                                  in_=b_scales[:, 4 * q:4 * q + 4, :].bitcast(I32))

        def load_b(h):
            words = b_words.rearrange("g p n t -> p g (n t)")
            for c in range(2):
                codes = keep.tile([P, 2, HALF], U32, name="b_codes%d_%d" % (h, c), align_bytes=64)
                nc.sync.dma_start(out=codes[:].bitcast(I32),
                                  in_=words[:, 2 * c:2 * c + 2, 4 * h * HALF:4 * (h + 1) * HALF].bitcast(I32))
                b_codes[h, c] = codes

        load_z(0, 0, 1)
        load_z(0, 1, 1)
        load_z(0, 2, 2)
        load_a_scales(0)
        load_a(0)
        load_a(1)
        load_z(1, 0, 2)
        load_a_scales(1)
        load_a(2)
        load_z(1, 2, 2)
        load_a(3)
        load_z(2, 0, PASSES)
        load_b_scales()
        load_b(0)
        load_b(1)
        load_z(3, 0, PASSES)
        for j in range(X_TILES):
            load_x(j)

        y_codes = [keep.tile([P, PASSES * P], U32, name="y_codes%d" % i, align_bytes=64) for i in range(Y_TILES)]
        y_scale = [keep.tile([P, PASSES * P], U8, name="y_scale%d" % i, align_bytes=64) for i in range(Y_TILES)]
        x_codes, x_scale = {}, {}
        for h in range(2):
            for g in range(PASSES):
                x_codes[h, g] = keep.tile([P, HALF], U32, name="x_codes%d_%d" % (h, g), align_bytes=64)
                x_scale[h, g] = keep.tile([P, HALF], U8, name="x_scale%d_%d" % (h, g), align_bytes=64)

        roots, y_sorted, x_sorted, turned, grouped, sums, partial = {}, {}, {}, {}, {}, {}, {}

        def bank_tile(shape, bank):
            return psum.tile(shape, F32, name="bank%d" % bank)

        def z_by_parity(i, g0, passes):
            raw, first = z_raw[i, g0]
            return raw[:, first * K_PASS:(first + passes) * K_PASS].rearrange("p (w u e) -> p u w e", u=2, e=2)

        def root(i, g0, passes, parities=(slice(0, 2),)):
            inverse = stage.tile([P, 2, passes * P, 2], F32, name="root", align_bytes=64)
            for u in parities:
                nc.scalar.activation(out=inverse[:, u], in_=z_by_parity(i, g0, passes)[:, u],
                                     func=ACT.Abs_reciprocal_sqrt)
            roots[i, g0] = inverse

        def power(i, g0, passes):
            y = stage.tile([P, 2, passes * P, 2], BF16, name="y_sorted", align_bytes=64)
            for u in range(2):
                nc.vector.scalar_tensor_tensor(out=y[:, u], in0=roots[i, g0][:, u], scalar=ROOT_CAP,
                                               in1=z_by_parity(i, g0, passes)[:, u], op0=ALU.min, op1=ALU.mult)
            y_sorted[i, g0] = y

        def sort_x(j):
            pairs = stage.tile([P, 2, PASSES * P], F32, name="x_sorted", align_bytes=64)
            nc.vector.tensor_copy(out=pairs[:], in_=x_raw[j][:].bitcast(F32).rearrange("p (w u) -> p u w", u=2))
            x_sorted[j] = pairs

        def turn(unit, bank):
            if unit[0] == "y":
                i, g0, passes = unit[1:]
                pairs = y_sorted[i, g0][:].rearrange("p u w e -> p u (w e)").bitcast(F32)
                blocks = [pairs[:, :, g * P:(g + 1) * P] for g in range(passes)]
            else:
                d, g = unit[1:]
                blocks = [x_sorted[j][:, :, g * P:(g + 1) * P] for j in (2 * d, 2 * d + 1)]
            tile = bank_tile([P, 2, 2, P], bank)
            for a, block in enumerate(blocks):
                for u in range(2):
                    nc.tensor.transpose(tile[:, a, u, :], block[:, u, :], ident[:])
            turned[unit] = (tile, len(blocks))

        def copy_out(unit):
            tile, count = turned[unit]
            pairs = stage.tile([P, count, P, 2], F32, name="grouped", bufs=6, align_bytes=64)
            nc.scalar.copy(out=pairs[:], in_=tile[:, 0:count].rearrange("p a u r -> p a r u"))
            grouped[unit] = pairs

        def quantize(unit):
            if unit[0] == "y":
                i, g0, passes = unit[1:]
                cols = slice(g0 * P, (g0 + passes) * P)
                codes, scale = y_codes[i], y_scale[i]
            else:
                d, g = unit[1:]
                cols = slice(d % 2 * 2 * P, (d % 2 + 1) * 2 * P)
                codes, scale = x_codes[d // 2, g], x_scale[d // 2, g]
            nc.vector.quantize_mx(out=codes[:, cols].bitcast(FP8X4), scales=scale[:, cols],
                                  in_=grouped[unit][:].rearrange("p a r u -> p (a r u)").bitcast(BF16))

        def multiply(acc, kind, i, h, passes, cols):
            for g in passes:
                if kind == "a":
                    codes = a_codes[g][:, 2 * h * HALF:2 * (h + 1) * HALF].bitcast(FP4X4)
                    scale = a_scale[g // 2][:, g % 2, h * HALF:(h + 1) * HALF]
                elif kind == "b":
                    codes = b_codes[h, g // 2][:, g % 2, :].bitcast(FP8X4)
                    scale = b_scale[4 * g:P, h * HALF:(h + 1) * HALF]
                else:
                    codes, scale = x_codes[h, g][:, cols].bitcast(FP8X4), x_scale[h, g][:, cols]
                y_cols = slice(g * P, (g + 1) * P)
                nc.tensor.matmul_mx(out=acc, lhsT=y_codes[i][:, y_cols].bitcast(FP8X4),
                                    lhsT_scale=y_scale[i][:, y_cols], rhs=codes, rhs_scale=scale,
                                    start=(g == 0), stop=(g == PASSES - 1))

        def product(group, bank, passes=range(PASSES)):
            if group not in sums:
                sums[group] = bank_tile([P, HALF], bank)
            multiply(sums[group][:], *group, passes, slice(0, HALF))

        def add_and_store(acc, i, h, cols):
            part = partial[i, h][:, cols]
            nc.vector.tensor_tensor(out=part, in0=acc, in1=part, op=ALU.add)
            nc.sync.dma_start(out=out[i * P:(i + 1) * P, h * HALF + cols.start:h * HALF + cols.stop], in_=part)

        def empty(group):
            kind, i, h = group
            if kind == "a":
                partial[i, h] = keep.tile([P, HALF], F32, name="partial%d_%d" % (i, h))
                nc.scalar.copy(out=partial[i, h][:], in_=sums[group][:])
            elif kind == "b":
                nc.vector.tensor_tensor(out=partial[i, h][:], in0=sums[group][:], in1=partial[i, h][:], op=ALU.mult)
            else:
                add_and_store(sums[group][:], i, h, slice(0, HALF))

        def a_passes(i, g):
            for h in range(2):
                product(("a", i, h), TURN_BANKS + 2 * i + h, [g])

        single = [(i, g, 1) for i in range(2) for g in range(PASSES)]
        units = [("y",) + chunk for chunk in single]
        root(*single[0], parities=(slice(0, 1), slice(1, 2)))
        power(*single[0])
        root(*single[1])
        turn(units[0], 0)
        power(*single[1])
        root(*single[2])
        turn(units[1], 1)
        copy_out(units[0])
        quantize(units[0])
        a_passes(0, 0)
        root(*single[3])
        power(*single[2])
        copy_out(units[1])
        quantize(units[1])
        power(*single[3])
        turn(units[2], 2)
        turn(units[3], 3)
        a_passes(0, 1)
        for n in range(4, len(single) + 1, 2):
            new, old = range(n, min(n + 2, len(single))), (n - 2, n - 1)
            for idx in new[:1]:
                root(*single[idx])
                power(*single[idx])
                root(*single[idx + 1])
            for idx in old:
                copy_out(units[idx])
            for idx in new[1:]:
                power(*single[idx])
            for idx in old:
                quantize(units[idx])
            for idx in new:
                turn(units[idx], single[idx][1])
            for idx in old:
                a_passes(*single[idx][:2])

        early, late = range(0, 2), range(2, PASSES)
        y2_units = [("y", 2, 0, 2), ("y", 2, 2, 2)]
        root(2, 0, 2)
        empty(("a", 0, 0))
        power(2, 0, 2)
        product(("b", 0, 0), 3, early)
        product(("b", 1, 0), 4, early)
        root(2, 2, 2)
        empty(("a", 0, 1))
        empty(("a", 1, 0))
        power(2, 2, 2)
        product(("b", 0, 0), 3, late)
        product(("b", 1, 0), 4, late)
        empty(("a", 1, 1))
        empty(("b", 0, 0))
        product(("b", 0, 1), 5, early)
        for unit in y2_units:
            turn(unit, unit[2])
        for unit in y2_units:
            copy_out(unit)
        empty(("b", 1, 0))
        product(("b", 1, 1), 6, early)
        product(("b", 0, 1), 5, late)
        product(("b", 1, 1), 6, late)
        for unit in y2_units:
            quantize(unit)
        root(3, 0, 2)
        root(3, 2, 2)
        empty(("b", 0, 1))
        empty(("b", 1, 1))
        power(3, 0, 2)
        power(3, 2, 2)

        taken = []

        def next_bank():
            taken.append(TURN_BANKS + (len(taken) - 1) % (BANKS - TURN_BANKS))
            return taken[-1]

        y3_units = [("y", 3, 0, 2), ("y", 3, 2, 2)]
        for h in range(2):
            product(("a", 2, h), next_bank())
            empty(("a", 2, h))
            sort_x(h)
        product(("b", 2, 0), next_bank())
        empty(("b", 2, 0))
        for unit in y3_units:
            turn(unit, unit[2])
        for unit in y3_units:
            copy_out(unit)
        product(("b", 2, 1), next_bank())
        for unit in y3_units:
            quantize(unit)
        empty(("b", 2, 1))

        groups = [(kind, 3, h) for kind in ("a", "b") for h in range(2)] + [("x", i, 0) for i in range(Y_TILES)]
        for d in range(X_TILES // 2):
            x_units = [("x", d, g) for g in range(PASSES)]
            for unit in x_units:
                turn(unit, unit[2])
            for j in range(2 * d + 2, min(2 * d + 4, X_TILES)):
                sort_x(j)
            for unit in x_units:
                copy_out(unit)
            for step in range(2):
                product(groups[2 * d + step], next_bank())
                for unit in x_units[2 * step:2 * step + 2]:
                    quantize(unit)
                empty(groups[2 * d + step])

        for i in range(LAST_PIECES[0][0]):
            product(("x", i, 1), next_bank())
            empty(("x", i, 1))
        for bank, (i, n0, width) in enumerate(LAST_PIECES):
            cols = slice(n0, n0 + width)
            acc = bank_tile([P, width], bank)
            multiply(acc[:], "x", i, 1, range(PASSES), cols)
            add_and_store(acc[:], i, 1, cols)
